import numpy as np
import ml_dtypes


def mxq(x, axis, fmt="e4m3"):
    dtype, down = {"e4m3": (ml_dtypes.float8_e4m3fn, 7), "e5m2": (ml_dtypes.float8_e5m2, 14)}[fmt]
    v = np.moveaxis(np.asarray(x, np.float32).astype(ml_dtypes.bfloat16).astype(np.float64), axis, -1)
    blocks = v.reshape(v.shape[:-1] + (-1, 32))
    amax = np.abs(blocks).max(-1, keepdims=True)
    byte = np.maximum(np.where(amax > 0, np.frexp(amax)[1] - 1 + 127, 0) - down, 1)
    scale = np.exp2(byte - 127.0)
    codes = (blocks / scale).astype(np.float32).astype(dtype).astype(np.float64)
    return np.moveaxis((codes * scale).reshape(v.shape), -1, axis)


WIDE = False


def mx_kscale(k):
    if not WIDE:
        return np.ones(k)
    levels = np.array([10, -10, 5, -5, 0])
    if k % 512:
        return np.exp2(np.random.permutation(np.resize(levels, k // 32))).repeat(32)
    a = np.empty((k // 512, 16))
    for p in range(k // 512):
        a[p, :8] = np.random.permutation(np.resize(levels, 8))
        for g in range(8):
            far = levels[np.abs(levels - a[p, g]) >= 10]
            a[p, g + 8] = far[np.random.randint(len(far))]
    return np.exp2(a.ravel()).repeat(32)


BF16 = ml_dtypes.bfloat16


def bf(x):
    return np.asarray(x, np.float32).astype(BF16)


def f64(x):
    return np.asarray(x).astype(np.float64)


E2M1 = np.array([0.0, 0.5, 1.0, 1.5, 2.0, 3.0, 4.0, 6.0, -0.0, -0.5, -1.0, -1.5, -2.0, -3.0, -4.0, -6.0])


def pack_weight(w, fmt):
    k, n = w.shape
    w = f64(bf(w)).reshape(k // 32, 32, n)
    amax = np.abs(w).max(1)
    if fmt == "e4m3":
        byte = np.frexp(amax)[1] - 1 + 127 - 7
    else:
        mant, ex = np.frexp(amax / 6.0)
        byte = np.where(mant > 0.5, ex, ex - 1) + 127
    byte = np.clip(np.where(amax > 0, byte, 1), 1, 254)
    scaled = (w * np.exp2(127.0 - byte)[:, None, :]).reshape(k, n).astype(np.float32)
    by_word = np.ascontiguousarray(scaled.reshape(k // 512, 128, 4, n).transpose(0, 1, 3, 2))
    if fmt == "e4m3":
        words = by_word.astype(ml_dtypes.float8_e4m3fn).view(np.uint8)
    else:
        c = by_word.astype(ml_dtypes.float4_e2m1fn).view(np.uint8) & 0xF
        words = c[..., 0::2] | (c[..., 1::2] << 4)
    return np.ascontiguousarray(words), np.ascontiguousarray(byte.astype(np.uint8).reshape(k // 512, 16, n))


def unpack_weight(words, scales, fmt):
    g, p, n, _ = words.shape
    if fmt == "e4m3":
        vals = np.ascontiguousarray(words).view(ml_dtypes.float8_e4m3fn).astype(np.float64)
    else:
        nib = np.empty((g, p, n, 4), np.uint8)
        nib[..., 0::2] = words & 0xF
        nib[..., 1::2] = words >> 4
        vals = E2M1[nib]
    vals = vals * np.repeat(np.exp2(scales.astype(np.float64) - 127.0), 8, axis=1)[..., None]
    return vals.transpose(0, 1, 3, 2).reshape(g * 512, n)
def pack4(w):
    words, scales = pack_weight(w, "e2m1")
    return words.reshape(words.shape[0], 128, -1), scales


def unpack4(words, scales):
    return unpack_weight(words.reshape(words.shape[0], 128, -1, 2), scales, "e2m1")


def planes(Y):
    n, m = Y.shape
    b = f64(bf(Y)).reshape(n // 32, 32, m)
    amax = np.abs(b).max(1)
    byte = np.clip(np.where(amax > 0, np.frexp(amax)[1] - 1 + 127 - 7, 1), 1, 254)
    codes = (b * np.exp2(127.0 - byte)[:, None, :]).reshape(n, m).astype(np.float32).astype(ml_dtypes.float8_e4m3fn).view(np.uint8)
    words = codes.reshape(n // 512, 128, 4, m).transpose(0, 1, 3, 2)
    return np.ascontiguousarray(words), np.ascontiguousarray(byte.astype(np.uint8).reshape(n // 512, 16, m))


M, K, N = 1536, 1024, 1024
GAMMA = 1.5
SHARES = (0.4, 0.3, 0.3)


def euler_weights(share, factor):
    t = np.exp(1.3 * np.random.randn(K, N))
    return share * t / t.sum(axis=0) * factor


def setup_inputs():
    s = mx_kscale(K)[:, None]
    sav = 0.4 * np.exp(0.5 * np.random.randn(M))
    cons = sav ** 0.3 * np.exp(0.6 * np.random.randn(K, M))
    factor = np.exp(0.9 * np.random.randn(N))
    u_words, u_scales = pack_weight(cons ** -GAMMA * s, "e4m3")
    calm_words, calm_scales = pack4(euler_weights(SHARES[0], factor) / s)
    boom_words, boom_scales = pack_weight(euler_weights(SHARES[1], factor) / s, "e4m3")
    slump = bf(euler_weights(SHARES[2], factor) / s)
    return {"u_words": u_words, "u_scales": u_scales,
            "calm_words": calm_words, "calm_scales": calm_scales,
            "boom_words": boom_words, "boom_scales": boom_scales,
            "slump": slump, "sav": bf(sav)}


def reference(u_words, u_scales, calm_words, calm_scales, boom_words, boom_scales, slump, sav):
    U = unpack_weight(u_words, u_scales, "e4m3")
    calm = unpack4(calm_words, calm_scales)
    boom = unpack_weight(boom_words, boom_scales, "e4m3")
    slump_q = mxq(f64(slump), 0, "e4m3")
    E = (U.T @ calm) + (U.T @ boom) + (U.T @ slump_q)
    y = f64(sav)[:, None] + E ** (-1.0 / GAMMA)
    Y = y.T
    words, scales = planes(Y)
    return y, words, scales

@@ -1,0 +1,298 @@
+from contextlib import ExitStack
+
+import concourse.mybir as mybir
+from concourse.masks import make_identity
+
+M, K, N = 1536, 1024, 1024
+GAMMA = 1.5
+FLOPS = 3 * 2 * M * K * N
+
+F32 = mybir.dt.float32
+BF16 = mybir.dt.bfloat16
+I32 = mybir.dt.int32
+U32 = mybir.dt.uint32
+U8 = mybir.dt.uint8
+FP8X4 = mybir.dt.float8_e4m3fn_x4
+FP4X4 = mybir.dt.float4_e2m1fn_x4
+ACT = mybir.ActivationFunctionType
+ADD = mybir.AluOpType.add
+
+P = 128
+PACK = 4
+PASSES = K // (P * PACK)
+WIDE = 512
+HALVES = N // WIDE
+M_TILES = M // P
+UNITS = HALVES * M_TILES
+QUADS = 4
+ROWS = 4
+BOOM_ROW = 4
+FIRST = 4
+GROUP = 6
+SUM_BANKS = 6
+TURN_BANKS = 2
+WARM = 9
+VECTOR_COLS = 336
+
+
+def tile_endogenous_gridpoint_euler_step_k3_kernel(
+    tc, u_words, u_scales, calm_words, calm_scales, boom_words, boom_scales, slump, sav, out_0, out_1, out_2
+):
+    nc = tc.nc
+    with ExitStack() as ctx:
+        keep = ctx.enter_context(tc.tile_pool(name="keep", bufs=1))
+        flow = ctx.enter_context(tc.tile_pool(name="flow", bufs=2))
+        psum = ctx.enter_context(tc.psum_pool(name="psum", bufs=1))
+        ctx.enter_context(tc.manual_schedule())
+
+        split = FIRST * P
+        u_spans = [(0, split), (split, M)]
+        u_code = [keep.tile([P, PASSES, b - a], U32, name="u_code%d" % i, align_bytes=64) for i, (a, b) in enumerate(u_spans)]
+        u_scale = [keep.tile([P, PASSES, b - a], U8, name="u_scale%d" % i, align_bytes=64) for i, (a, b) in enumerate(u_spans)]
+        calm_code = [keep.tile([P, PASSES, 2 * WIDE], U8, name="calm_code%d" % h, align_bytes=64) for h in range(HALVES)]
+        boom_code = [keep.tile([P, PASSES, WIDE], U32, name="boom_code%d" % h, align_bytes=64) for h in range(HALVES)]
+        given_scale = keep.tile([P, PASSES, N], U8, align_bytes=64)
+        slump_raw = {}
+        slump_code = {}
+        slump_scale = {}
+        for h in range(HALVES):
+            for g in range(PASSES):
+                slump_raw[h, g] = keep.tile([P, PACK, WIDE], BF16, name="slump_raw%d%d" % (h, g), align_bytes=64)
+                slump_code[h, g] = keep.tile([P, WIDE], U32, name="slump_code%d%d" % (h, g), align_bytes=64)
+                slump_scale[h, g] = keep.tile([P, WIDE], U8, name="slump_scale%d%d" % (h, g), align_bytes=64)
+        y_code = keep.tile([P, HALVES, M], U32, align_bytes=64)
+        y_scale = keep.tile([P, HALVES, M], U8, align_bytes=64)
+        ident = keep.tile([P, P], F32, align_bytes=64)
+        picker = keep.tile([P, 16], BF16, align_bytes=64)
+        sav_rows = keep.tile([P, P], BF16, align_bytes=64)
+        sav_col = keep.tile([P, 16], F32, align_bytes=64)
+        zeros = keep.tile([P, WIDE], BF16, align_bytes=64)
+        one = keep.tile([P, 1], F32, align_bytes=64)
+        spare = keep.tile([P, 1], F32, align_bytes=64)
+
+        def bank(b):
+            return psum.tile([P, WIDE], F32, name="bank%d" % b, tag="bank%d" % b)
+
+        def words(ap):
+            return ap.bitcast(I32)
+
+        def load_u_codes(i):
+            a, b = u_spans[i]
+            src = u_words.rearrange("g p m t -> p g (m t)")[:, :, PACK * a : PACK * b]
+            nc.sync.dma_start(out=words(u_code[i][:]), in_=words(src))
+
+        def load_calm_codes(h):
+            src = calm_words.rearrange("g p b -> p g b")[:, :, 2 * WIDE * h : 2 * WIDE * (h + 1)]
+            nc.sync.dma_start(out=words(calm_code[h][:]), in_=words(src))
+
+        def load_boom_codes(h):
+            src = boom_words.rearrange("g p n t -> p g (n t)")[:, :, PACK * WIDE * h : PACK * WIDE * (h + 1)]
+            nc.sync.dma_start(out=words(boom_code[h][:]), in_=words(src))
+
+        def load_slump(h, g):
+            src = slump[P * PACK * g : P * PACK * (g + 1), WIDE * h : WIDE * (h + 1)]
+            nc.sync.dma_start(out=slump_raw[h, g][:], in_=src.rearrange("(p j) n -> p j n", j=PACK))
+
+        def load_scales(queue, plane, row, cols, scales, src_cols):
+            for q in range(QUADS):
+                src = scales[:, ROWS * q : ROWS * (q + 1), src_cols].rearrange("g r n -> r g n")
+                top = 32 * q + row
+                queue.dma_start(out=words(plane[top : top + ROWS, :, cols]), in_=words(src))
+
+        def interleave_slump(h, g, shared):
+            grouped = flow.tile([P, WIDE, PACK], BF16, name="slump_grouped", align_bytes=64)
+            src = slump_raw[h, g][:].rearrange("p j n -> p n j")
+            cut = VECTOR_COLS if shared else WIDE
+            nc.vector.tensor_copy(out=grouped[:, :cut, :], in_=src[:, :cut, :])
+            if shared:
+                nc.scalar.copy(out=grouped[:, cut:, :], in_=src[:, cut:, :])
+            return grouped
+
+        def quantise_slump(h, g, grouped):
+            nc.vector.quantize_mx(
+                out=slump_code[h, g][:].bitcast(FP8X4),
+                scales=slump_scale[h, g][:],
+                in_=grouped[:].rearrange("p n j -> p (n j)"),
+            )
+
+        sums = {}
+
+        def one_pass(unit, regime, g, start, stop):
+            h, i = divmod(unit, M_TILES)
+            part = 0 if i < FIRST else 1
+            lo = i * P - u_spans[part][0]
+            cols = slice(WIDE * h, WIDE * (h + 1))
+            if regime == "calm":
+                rhs, rhs_scale = calm_code[h][:, g, :].bitcast(FP4X4), given_scale[:, g, cols]
+            elif regime == "boom":
+                rhs, rhs_scale = boom_code[h][:, g, :].bitcast(FP8X4), given_scale[BOOM_ROW:, g, cols]
+            else:
+                rhs, rhs_scale = slump_code[h, g][:].bitcast(FP8X4), slump_scale[h, g][:]
+            if start:
+                sums[unit] = bank(unit % SUM_BANKS)
+            nc.tensor.matmul_mx(
+                out=sums[unit][:],
+                lhsT=u_code[part][:, g, lo : lo + P].bitcast(FP8X4),
+                lhsT_scale=u_scale[part][:, g, lo : lo + P],
+                rhs=rhs,
+                rhs_scale=rhs_scale,
+                start=start,
+                stop=stop,
+            )
+
+        steps = [(regime, g) for regime in ("calm", "boom", "slump") for g in range(PASSES)]
+
+        def multiply(unit):
+            for s, (regime, g) in enumerate(steps):
+                one_pass(unit, regime, g, s == 0, s == len(steps) - 1)
+
+        logs = {}
+        cons = {}
+        halfs = {}
+        turned = {}
+        packed = {}
+
+        def take_log(unit):
+            logs[unit] = flow.tile([P, WIDE], F32, name="log_e", bufs=GROUP + 1)
+            nc.scalar.activation(out=logs[unit][:], in_=sums[unit][:], func=ACT.Ln)
+
+        def take_exp(unit):
+            cons[unit] = flow.tile([P, WIDE], F32, name="cons", bufs=GROUP)
+            nc.scalar.activation(out=cons[unit][:], in_=logs[unit][:], func=ACT.Exp, scale=-1.0 / GAMMA)
+
+        def round_y(unit):
+            pair, a = divmod(unit, 2)
+            i = unit % M_TILES
+            if a == 0:
+                halfs[pair] = flow.tile([P, 2, 2, P, 2], BF16, name="y_bf16", bufs=6, align_bytes=64)
+            nc.vector.tensor_scalar(
+                out=halfs[pair][:, a],
+                in0=cons[unit][:].rearrange("m (p u e) -> m u p e", u=2, e=2),
+                scalar1=sav_col[:, i : i + 1],
+                scalar2=None,
+                op0=ADD,
+            )
+
+        def store_y(unit, on_scalar):
+            h, i = divmod(unit, M_TILES)
+            y = flow.tile([P, WIDE], F32, name="y", bufs=6)
+            if on_scalar:
+                nc.scalar.activation(out=y[:], in_=cons[unit][:], func=ACT.Identity, bias=sav_col[:, i : i + 1])
+            else:
+                nc.vector.tensor_scalar(out=y[:], in0=cons[unit][:], scalar1=sav_col[:, i : i + 1], scalar2=None, op0=ADD)
+            nc.sync.dma_start(out=out_0[P * i : P * (i + 1), WIDE * h : WIDE * (h + 1)], in_=y[:])
+
+        def turn(pair):
+            turned[pair] = bank(SUM_BANKS + pair % TURN_BANKS)
+            src = halfs[pair][:].rearrange("m a u p e -> m (a u p e)").bitcast(F32)
+            for s in range(4):
+                nc.tensor.transpose(turned[pair][:, P * s : P * (s + 1)], src[:, P * s : P * (s + 1)], ident[:])
+
+        def gather(pair, on_scalar):
+            packed[pair] = flow.tile([P, 2 * P * PACK], BF16, name="y_packed", bufs=3, align_bytes=64)
+            dst = packed[pair][:].bitcast(F32).rearrange("p (a m u) -> p a m u", a=2, u=2)
+            src = turned[pair][:].rearrange("p (a u m) -> p a m u", a=2, u=2)
+            if on_scalar:
+                nc.scalar.copy(out=dst, in_=src)
+            else:
+                nc.vector.tensor_copy(out=dst, in_=src)
+
+        def quantise_y(pair):
+            h, j = divmod(pair, M_TILES // 2)
+            cols = slice(2 * P * j, 2 * P * (j + 1))
+            nc.vector.quantize_mx(out=y_code[:, h, cols].bitcast(FP8X4), scales=y_scale[:, h, cols], in_=packed[pair][:])
+            dst = out_1[h].rearrange("p m t -> p (m t)")[:, PACK * cols.start : PACK * cols.stop]
+            nc.sync.dma_start(out=words(dst), in_=words(y_code[:, h, cols]))
+            if j == M_TILES // 2 - 1:
+                for q in range(QUADS):
+                    nc.sync.dma_start(
+                        out=words(out_2[h, ROWS * q : ROWS * (q + 1), :]),
+                        in_=words(y_scale[32 * q : 32 * q + ROWS, h, :]),
+                    )
+
+        def finish(pairs):
+            for pair in pairs:
+                turn(pair)
+            for pair in pairs:
+                gather(pair, False)
+            for pair in pairs:
+                quantise_y(pair)
+
+        nc.vector.memset(words(u_scale[0][:]), 0)
+        nc.vector.memset(words(given_scale[:]), 0)
+        nc.vector.memset(zeros[:], 0.0)
+        nc.vector.memset(one[:], 1.0)
+        nc.vector.memset(sav_rows[:], 0.0)
+        nc.vector.memset(words(u_scale[1][:]), 0)
+
+        load_u_codes(0)
+        load_calm_codes(0)
+        load_scales(nc.sync, u_scale[0], 0, slice(0, split), u_scales, slice(0, split))
+        load_scales(nc.scalar, given_scale, 0, slice(0, WIDE), calm_scales, slice(0, WIDE))
+        nc.scalar.activation(out=spare[:], in_=one[:], func=ACT.Ln)
+        load_boom_codes(0)
+        load_slump(0, 0)
+        load_scales(nc.sync, given_scale, BOOM_ROW, slice(0, N), boom_scales, slice(0, N))
+        load_slump(0, 1)
+        nc.gpsimd.dma_start(out=sav_rows[:M_TILES, :], in_=sav.rearrange("(i p) -> i p", p=P))
+        load_u_codes(1)
+        load_scales(nc.sync, u_scale[1], 0, slice(0, M - split), u_scales, slice(split, M))
+        load_scales(nc.sync, given_scale, 0, slice(WIDE, N), calm_scales, slice(WIDE, N))
+        load_calm_codes(1)
+        load_boom_codes(1)
+        load_slump(1, 0)
+        load_slump(1, 1)
+        make_identity(nc, ident[:])
+
+        warm = bank(SUM_BANKS + 1)
+        for w in range(WARM):
+            nc.tensor.matmul(warm[:], lhsT=zeros[:, :P], rhs=zeros[:], start=True, stop=True)
+
+        for g in range(PASSES):
+            quantise_slump(0, g, interleave_slump(0, g, True))
+        nc.vector.tensor_copy(out=picker[:], in_=ident[:, :16])
+
+        for s, (regime, g) in enumerate(steps):
+            for unit in range(FIRST):
+                one_pass(unit, regime, g, s == 0, s == len(steps) - 1)
+                if s == len(steps) - 1:
+                    take_log(unit)
+        spread = bank(SUM_BANKS)
+        nc.tensor.matmul(spread[:, :16], lhsT=sav_rows[:], rhs=picker[:], start=True, stop=True)
+        nc.vector.tensor_copy(out=sav_col[:], in_=spread[:, :16])
+
+        quantise_slump(1, 0, interleave_slump(1, 0, False))
+
+        groups = UNITS // GROUP
+        waiting = []
+        for k in range(groups):
+            units = range(k * GROUP, (k + 1) * GROUP)
+            last = k == groups - 1
+            for j, unit in enumerate(units):
+                if unit >= FIRST:
+                    multiply(unit)
+                    take_log(unit)
+                if waiting and not last and j in (3, 5):
+                    finish(waiting[:2])
+                    waiting = waiting[2:]
+            if last:
+                finish(waiting[:2])
+                finish(waiting[2:])
+                for j, unit in enumerate(units):
+                    take_exp(unit)
+                    round_y(unit)
+                    if j < 3:
+                        store_y(unit, False)
+                    if j in (3, 5):
+                        finish([unit // 2 - 1])
+                for unit in units[3:]:
+                    store_y(unit, True)
+                finish([UNITS // 2 - 1])
+            else:
+                for unit in units:
+                    take_exp(unit)
+                    round_y(unit)
+                    store_y(unit, False)
+                waiting = [unit // 2 for unit in units[1::2]]
+                if k == 0:
+                    quantise_slump(1, 1, interleave_slump(1, 1, False))

@@ -26,12 +26,11 @@ M_TILES = M // P
 UNITS = HALVES * M_TILES
 QUADS = 4
 ROWS = 4
-BOOM_ROW = 4
 FIRST = 4
 GROUP = 6
 SUM_BANKS = 6
 TURN_BANKS = 2
-WARM = 9
+WARM = 7
 VECTOR_COLS = 336
 
 
@@ -48,10 +47,11 @@ def tile_endogenous_gridpoint_euler_step_k3_kernel(
         split = FIRST * P
         u_spans = [(0, split), (split, M)]
         u_code = [keep.tile([P, PASSES, b - a], U32, name="u_code%d" % i, align_bytes=64) for i, (a, b) in enumerate(u_spans)]
-        u_scale = [keep.tile([P, PASSES, b - a], U8, name="u_scale%d" % i, align_bytes=64) for i, (a, b) in enumerate(u_spans)]
+        u_scale = keep.tile([P, PASSES, M], U8, align_bytes=64)
         calm_code = [keep.tile([P, PASSES, 2 * WIDE], U8, name="calm_code%d" % h, align_bytes=64) for h in range(HALVES)]
         boom_code = [keep.tile([P, PASSES, WIDE], U32, name="boom_code%d" % h, align_bytes=64) for h in range(HALVES)]
-        given_scale = keep.tile([P, PASSES, N], U8, align_bytes=64)
+        calm_scale = keep.tile([P, PASSES, N], U8, align_bytes=64)
+        boom_scale = keep.tile([P, PASSES, N], U8, align_bytes=64)
         slump_raw = {}
         slump_code = {}
         slump_scale = {}
@@ -93,11 +93,10 @@ def tile_endogenous_gridpoint_euler_step_k3_kernel(
             src = slump[P * PACK * g : P * PACK * (g + 1), WIDE * h : WIDE * (h + 1)]
             nc.sync.dma_start(out=slump_raw[h, g][:], in_=src.rearrange("(p j) n -> p j n", j=PACK))
 
-        def load_scales(queue, plane, row, cols, scales, src_cols):
-            for q in range(QUADS):
-                src = scales[:, ROWS * q : ROWS * (q + 1), src_cols].rearrange("g r n -> r g n")
-                top = 32 * q + row
-                queue.dma_start(out=words(plane[top : top + ROWS, :, cols]), in_=words(src))
+        def load_scales(queue, plane, scales):
+            rows = scales.rearrange("g (q r) n -> r q g n", r=ROWS)
+            for r in range(ROWS):
+                queue.dma_start(out=words(plane[r:P:32, :, :]), in_=words(rows[r]))
 
         def interleave_slump(h, g, shared):
             grouped = flow.tile([P, WIDE, PACK], BF16, name="slump_grouped", align_bytes=64)
@@ -123,9 +122,9 @@ def tile_endogenous_gridpoint_euler_step_k3_kernel(
             lo = i * P - u_spans[part][0]
             cols = slice(WIDE * h, WIDE * (h + 1))
             if regime == "calm":
-                rhs, rhs_scale = calm_code[h][:, g, :].bitcast(FP4X4), given_scale[:, g, cols]
+                rhs, rhs_scale = calm_code[h][:, g, :].bitcast(FP4X4), calm_scale[:, g, cols]
             elif regime == "boom":
-                rhs, rhs_scale = boom_code[h][:, g, :].bitcast(FP8X4), given_scale[BOOM_ROW:, g, cols]
+                rhs, rhs_scale = boom_code[h][:, g, :].bitcast(FP8X4), boom_scale[:, g, cols]
             else:
                 rhs, rhs_scale = slump_code[h, g][:].bitcast(FP8X4), slump_scale[h, g][:]
             if start:
@@ -133,14 +132,14 @@ def tile_endogenous_gridpoint_euler_step_k3_kernel(
             nc.tensor.matmul_mx(
                 out=sums[unit][:],
                 lhsT=u_code[part][:, g, lo : lo + P].bitcast(FP8X4),
-                lhsT_scale=u_scale[part][:, g, lo : lo + P],
+                lhsT_scale=u_scale[:, g, i * P : (i + 1) * P],
                 rhs=rhs,
                 rhs_scale=rhs_scale,
                 start=start,
                 stop=stop,
             )
 
-        steps = [(regime, g) for regime in ("calm", "boom", "slump") for g in range(PASSES)]
+        steps = [("slump", 0), ("calm", 0), ("calm", 1), ("boom", 0), ("boom", 1), ("slump", 1)]
 
         def multiply(unit):
             for s, (regime, g) in enumerate(steps):
@@ -173,71 +172,70 @@ def tile_endogenous_gridpoint_euler_step_k3_kernel(
                 op0=ADD,
             )
 
-        def store_y(unit, on_scalar):
+        def store_y(unit):
             h, i = divmod(unit, M_TILES)
             y = flow.tile([P, WIDE], F32, name="y", bufs=6)
-            if on_scalar:
-                nc.scalar.activation(out=y[:], in_=cons[unit][:], func=ACT.Identity, bias=sav_col[:, i : i + 1])
-            else:
-                nc.vector.tensor_scalar(out=y[:], in0=cons[unit][:], scalar1=sav_col[:, i : i + 1], scalar2=None, op0=ADD)
+            nc.vector.tensor_scalar(out=y[:], in0=cons[unit][:], scalar1=sav_col[:, i : i + 1], scalar2=None, op0=ADD)
             nc.sync.dma_start(out=out_0[P * i : P * (i + 1), WIDE * h : WIDE * (h + 1)], in_=y[:])
 
-        def turn(pair):
-            turned[pair] = bank(SUM_BANKS + pair % TURN_BANKS)
-            src = halfs[pair][:].rearrange("m a u p e -> m (a u p e)").bitcast(F32)
-            for s in range(4):
-                nc.tensor.transpose(turned[pair][:, P * s : P * (s + 1)], src[:, P * s : P * (s + 1)], ident[:])
+        def turn(batch, b):
+            turned[batch] = bank(b)
+            for a, unit in enumerate(batch):
+                src = halfs[unit // 2][:, unit % 2].rearrange("m u p e -> m (u p e)").bitcast(F32)
+                for u in range(2):
+                    s = 2 * a + u
+                    nc.tensor.transpose(turned[batch][:, P * s : P * (s + 1)], src[:, P * u : P * (u + 1)], ident[:])
 
-        def gather(pair, on_scalar):
-            packed[pair] = flow.tile([P, 2 * P * PACK], BF16, name="y_packed", bufs=3, align_bytes=64)
-            dst = packed[pair][:].bitcast(F32).rearrange("p (a m u) -> p a m u", a=2, u=2)
-            src = turned[pair][:].rearrange("p (a u m) -> p a m u", a=2, u=2)
+        def gather(batch, on_scalar):
+            count = len(batch)
+            packed[batch] = flow.tile([P, count * P * PACK], BF16, name="y_packed", bufs=4, align_bytes=64)
+            dst = packed[batch][:].bitcast(F32).rearrange("p (a m u) -> p a m u", a=count, u=2)
+            src = turned[batch][:, : count * 2 * P].rearrange("p (a u m) -> p a m u", a=count, u=2)
             if on_scalar:
                 nc.scalar.copy(out=dst, in_=src)
             else:
                 nc.vector.tensor_copy(out=dst, in_=src)
 
-        def quantise_y(pair):
-            h, j = divmod(pair, M_TILES // 2)
-            cols = slice(2 * P * j, 2 * P * (j + 1))
-            nc.vector.quantize_mx(out=y_code[:, h, cols].bitcast(FP8X4), scales=y_scale[:, h, cols], in_=packed[pair][:])
-            dst = out_1[h].rearrange("p m t -> p (m t)")[:, PACK * cols.start : PACK * cols.stop]
-            nc.sync.dma_start(out=words(dst), in_=words(y_code[:, h, cols]))
-            if j == M_TILES // 2 - 1:
-                for q in range(QUADS):
-                    nc.sync.dma_start(
-                        out=words(out_2[h, ROWS * q : ROWS * (q + 1), :]),
-                        in_=words(y_scale[32 * q : 32 * q + ROWS, h, :]),
-                    )
+        def quantise_y(batch):
+            h, i = divmod(batch[0], M_TILES)
+            cols = slice(P * i, P * (i + len(batch)))
+            nc.vector.quantize_mx(out=y_code[:, h, cols].bitcast(FP8X4), scales=y_scale[:, h, cols], in_=packed[batch][:])
+            if batch[-1] % 2 == 1:
+                lo = cols.stop - 2 * P
+                dst = out_1[h].rearrange("p m t -> p (m t)")[:, PACK * lo : PACK * cols.stop]
+                nc.sync.dma_start(out=words(dst), in_=words(y_code[:, h, lo : cols.stop]))
+            if cols.stop == M:
+                rows = out_2[h].rearrange("(q r) m -> r q m", r=ROWS)
+                for r in range(ROWS):
+                    queue = nc.scalar if h == HALVES - 1 and r % 2 == 0 else nc.sync
+                    queue.dma_start(out=words(rows[r]), in_=words(y_scale[r:P:32, h, :]))
 
-        def finish(pairs):
-            for pair in pairs:
-                turn(pair)
-            for pair in pairs:
-                gather(pair, False)
-            for pair in pairs:
-                quantise_y(pair)
+        def finish(batches):
+            for b, batch in enumerate(batches):
+                turn(batch, SUM_BANKS + b)
+            for batch in batches:
+                gather(batch, False)
+            for batch in batches:
+                quantise_y(batch)
 
-        nc.vector.memset(words(u_scale[0][:]), 0)
-        nc.vector.memset(words(given_scale[:]), 0)
+        nc.gpsimd.memset(words(u_scale[:]), 0)
+        nc.vector.memset(words(calm_scale[:]), 0)
         nc.vector.memset(zeros[:], 0.0)
         nc.vector.memset(one[:], 1.0)
+        nc.vector.memset(words(boom_scale[:]), 0)
         nc.vector.memset(sav_rows[:], 0.0)
-        nc.vector.memset(words(u_scale[1][:]), 0)
 
-        load_u_codes(0)
-        load_calm_codes(0)
-        load_scales(nc.sync, u_scale[0], 0, slice(0, split), u_scales, slice(0, split))
-        load_scales(nc.scalar, given_scale, 0, slice(0, WIDE), calm_scales, slice(0, WIDE))
-        nc.scalar.activation(out=spare[:], in_=one[:], func=ACT.Ln)
-        load_boom_codes(0)
         load_slump(0, 0)
-        load_scales(nc.sync, given_scale, BOOM_ROW, slice(0, N), boom_scales, slice(0, N))
+        load_u_codes(0)
+        load_scales(nc.scalar, u_scale, u_scales)
+        nc.scalar.activation(out=spare[:], in_=one[:], func=ACT.Ln)
+        load_calm_codes(0)
+        load_scales(nc.sync, calm_scale, calm_scales)
+        load_boom_codes(0)
+        load_scales(nc.sync, boom_scale, boom_scales)
         load_slump(0, 1)
         nc.gpsimd.dma_start(out=sav_rows[:M_TILES, :], in_=sav.rearrange("(i p) -> i p", p=P))
         load_u_codes(1)
-        load_scales(nc.sync, u_scale[1], 0, slice(0, M - split), u_scales, slice(split, M))
-        load_scales(nc.sync, given_scale, 0, slice(WIDE, N), calm_scales, slice(WIDE, N))
         load_calm_codes(1)
         load_boom_codes(1)
         load_slump(1, 0)
@@ -278,21 +276,22 @@ def tile_endogenous_gridpoint_euler_step_k3_kernel(
             if last:
                 finish(waiting[:2])
                 finish(waiting[2:])
-                for j, unit in enumerate(units):
+                tail = [tuple(units[0:2]), tuple(units[2:4]), (units[4],), (units[5],)]
+                for unit in units:
                     take_exp(unit)
                     round_y(unit)
-                    if j < 3:
-                        store_y(unit, False)
-                    if j in (3, 5):
-                        finish([unit // 2 - 1])
-                for unit in units[3:]:
-                    store_y(unit, True)
-                finish([UNITS // 2 - 1])
+                    for b, batch in enumerate(tail):
+                        if batch[-1] == unit:
+                            turn(batch, b)
+                    store_y(unit)
+                for batch in tail:
+                    gather(batch, True)
+                    quantise_y(batch)
             else:
                 for unit in units:
                     take_exp(unit)
                     round_y(unit)
-                    store_y(unit, False)
-                waiting = [unit // 2 for unit in units[1::2]]
+                    store_y(unit)
+                waiting = [(unit - 1, unit) for unit in units[1::2]]
                 if k == 0:
                     quantise_slump(1, 1, interleave_slump(1, 1, False))

@@ -26,10 +26,10 @@ M_TILES = M // P
 UNITS = HALVES * M_TILES
 QUADS = 4
 ROWS = 4
-FIRST = 4
+FIRST = 6
 GROUP = 6
-SUM_BANKS = 6
-TURN_BANKS = 2
+BANKS = 8
+TURN_AFTER = 4
 WARM = 7
 VECTOR_COLS = 336
 
@@ -41,16 +41,16 @@ def tile_endogenous_gridpoint_euler_step_k3_kernel(
     with ExitStack() as ctx:
         keep = ctx.enter_context(tc.tile_pool(name="keep", bufs=1))
         flow = ctx.enter_context(tc.tile_pool(name="flow", bufs=2))
-        psum = ctx.enter_context(tc.psum_pool(name="psum", bufs=1))
+        psum = ctx.enter_context(tc.psum_pool(name="psum", bufs=BANKS))
         ctx.enter_context(tc.manual_schedule())
 
         split = FIRST * P
         u_spans = [(0, split), (split, M)]
         u_code = [keep.tile([P, PASSES, b - a], U32, name="u_code%d" % i, align_bytes=64) for i, (a, b) in enumerate(u_spans)]
-        u_scale = keep.tile([P, PASSES, M], U8, align_bytes=64)
+        u_scale = [keep.tile([P, PASSES, b - a], U8, name="u_scale%d" % i, align_bytes=64) for i, (a, b) in enumerate(u_spans)]
         calm_code = [keep.tile([P, PASSES, 2 * WIDE], U8, name="calm_code%d" % h, align_bytes=64) for h in range(HALVES)]
         boom_code = [keep.tile([P, PASSES, WIDE], U32, name="boom_code%d" % h, align_bytes=64) for h in range(HALVES)]
-        calm_scale = keep.tile([P, PASSES, N], U8, align_bytes=64)
+        calm_scale = [keep.tile([P, PASSES, WIDE], U8, name="calm_scale%d" % h, align_bytes=64) for h in range(HALVES)]
         boom_scale = keep.tile([P, PASSES, N], U8, align_bytes=64)
         slump_raw = {}
         slump_code = {}
@@ -70,16 +70,16 @@ def tile_endogenous_gridpoint_euler_step_k3_kernel(
         one = keep.tile([P, 1], F32, align_bytes=64)
         spare = keep.tile([P, 1], F32, align_bytes=64)
 
-        def bank(b):
-            return psum.tile([P, WIDE], F32, name="bank%d" % b, tag="bank%d" % b)
+        def bank():
+            return psum.tile([P, WIDE], F32, name="bank")
 
         def words(ap):
             return ap.bitcast(I32)
 
-        def load_u_codes(i):
+        def load_u_codes(i, passes):
             a, b = u_spans[i]
-            src = u_words.rearrange("g p m t -> p g (m t)")[:, :, PACK * a : PACK * b]
-            nc.sync.dma_start(out=words(u_code[i][:]), in_=words(src))
+            src = u_words.rearrange("g p m t -> p g (m t)")[:, passes, PACK * a : PACK * b]
+            nc.sync.dma_start(out=words(u_code[i][:, passes, :]), in_=words(src))
 
         def load_calm_codes(h):
             src = calm_words.rearrange("g p b -> p g b")[:, :, 2 * WIDE * h : 2 * WIDE * (h + 1)]
@@ -122,24 +122,24 @@ def tile_endogenous_gridpoint_euler_step_k3_kernel(
             lo = i * P - u_spans[part][0]
             cols = slice(WIDE * h, WIDE * (h + 1))
             if regime == "calm":
-                rhs, rhs_scale = calm_code[h][:, g, :].bitcast(FP4X4), calm_scale[:, g, cols]
+                rhs, rhs_scale = calm_code[h][:, g, :].bitcast(FP4X4), calm_scale[h][:, g, :]
             elif regime == "boom":
                 rhs, rhs_scale = boom_code[h][:, g, :].bitcast(FP8X4), boom_scale[:, g, cols]
             else:
                 rhs, rhs_scale = slump_code[h, g][:].bitcast(FP8X4), slump_scale[h, g][:]
             if start:
-                sums[unit] = bank(unit % SUM_BANKS)
+                sums[unit] = bank()
             nc.tensor.matmul_mx(
                 out=sums[unit][:],
                 lhsT=u_code[part][:, g, lo : lo + P].bitcast(FP8X4),
-                lhsT_scale=u_scale[:, g, i * P : (i + 1) * P],
+                lhsT_scale=u_scale[part][:, g, lo : lo + P],
                 rhs=rhs,
                 rhs_scale=rhs_scale,
                 start=start,
                 stop=stop,
             )
 
-        steps = [("slump", 0), ("calm", 0), ("calm", 1), ("boom", 0), ("boom", 1), ("slump", 1)]
+        steps = [(regime, g) for regime in ("calm", "boom", "slump") for g in range(PASSES)]
 
         def multiply(unit):
             for s, (regime, g) in enumerate(steps):
@@ -178,8 +178,8 @@ def tile_endogenous_gridpoint_euler_step_k3_kernel(
             nc.vector.tensor_scalar(out=y[:], in0=cons[unit][:], scalar1=sav_col[:, i : i + 1], scalar2=None, op0=ADD)
             nc.sync.dma_start(out=out_0[P * i : P * (i + 1), WIDE * h : WIDE * (h + 1)], in_=y[:])
 
-        def turn(batch, b):
-            turned[batch] = bank(b)
+        def turn(batch):
+            turned[batch] = bank()
             for a, unit in enumerate(batch):
                 src = halfs[unit // 2][:, unit % 2].rearrange("m u p e -> m (u p e)").bitcast(F32)
                 for u in range(2):
@@ -211,38 +211,44 @@ def tile_endogenous_gridpoint_euler_step_k3_kernel(
                     queue.dma_start(out=words(rows[r]), in_=words(y_scale[r:P:32, h, :]))
 
         def finish(batches):
+            for batch in batches:
+                turn(batch)
             for b, batch in enumerate(batches):
-                turn(batch, SUM_BANKS + b)
-            for batch in batches:
                 gather(batch, False)
-            for batch in batches:
-                quantise_y(batch)
+                if b > 0:
+                    quantise_y(batches[b - 1])
+            quantise_y(batches[-1])
 
-        nc.gpsimd.memset(words(u_scale[:]), 0)
-        nc.vector.memset(words(calm_scale[:]), 0)
+        nc.gpsimd.memset(words(u_scale[0][:]), 0)
+        nc.vector.memset(words(calm_scale[0][:]), 0)
         nc.vector.memset(zeros[:], 0.0)
         nc.vector.memset(one[:], 1.0)
         nc.vector.memset(words(boom_scale[:]), 0)
         nc.vector.memset(sav_rows[:], 0.0)
+        nc.vector.memset(words(u_scale[1][:]), 0)
+        nc.vector.memset(words(calm_scale[1][:]), 0)
 
-        load_slump(0, 0)
-        load_u_codes(0)
-        load_scales(nc.scalar, u_scale, u_scales)
+        load_scales(nc.scalar, u_scale[0], u_scales[:, :, :split])
         nc.scalar.activation(out=spare[:], in_=one[:], func=ACT.Ln)
+        load_u_codes(0, slice(0, 1))
         load_calm_codes(0)
-        load_scales(nc.sync, calm_scale, calm_scales)
+        load_scales(nc.sync, calm_scale[0], calm_scales[:, :, :WIDE])
+        load_u_codes(0, slice(1, 2))
         load_boom_codes(0)
+        load_slump(0, 0)
         load_scales(nc.sync, boom_scale, boom_scales)
         load_slump(0, 1)
         nc.gpsimd.dma_start(out=sav_rows[:M_TILES, :], in_=sav.rearrange("(i p) -> i p", p=P))
-        load_u_codes(1)
+        load_u_codes(1, slice(0, PASSES))
+        load_scales(nc.sync, u_scale[1], u_scales[:, :, split:])
+        load_scales(nc.sync, calm_scale[1], calm_scales[:, :, WIDE:])
         load_calm_codes(1)
         load_boom_codes(1)
         load_slump(1, 0)
         load_slump(1, 1)
         make_identity(nc, ident[:])
 
-        warm = bank(SUM_BANKS + 1)
+        warm = bank()
         for w in range(WARM):
             nc.tensor.matmul(warm[:], lhsT=zeros[:, :P], rhs=zeros[:], start=True, stop=True)
 
@@ -250,12 +256,14 @@ def tile_endogenous_gridpoint_euler_step_k3_kernel(
             quantise_slump(0, g, interleave_slump(0, g, True))
         nc.vector.tensor_copy(out=picker[:], in_=ident[:, :16])
 
-        for s, (regime, g) in enumerate(steps):
+        for s, (regime, g) in enumerate(steps[:-PASSES]):
             for unit in range(FIRST):
-                one_pass(unit, regime, g, s == 0, s == len(steps) - 1)
-                if s == len(steps) - 1:
-                    take_log(unit)
-        spread = bank(SUM_BANKS)
+                one_pass(unit, regime, g, s == 0, False)
+        for unit in range(FIRST):
+            for g in range(PASSES):
+                one_pass(unit, "slump", g, False, g == PASSES - 1)
+            take_log(unit)
+        spread = bank()
         nc.tensor.matmul(spread[:, :16], lhsT=sav_rows[:], rhs=picker[:], start=True, stop=True)
         nc.vector.tensor_copy(out=sav_col[:], in_=spread[:, :16])
 
@@ -270,20 +278,20 @@ def tile_endogenous_gridpoint_euler_step_k3_kernel(
                 if unit >= FIRST:
                     multiply(unit)
                     take_log(unit)
-                if waiting and not last and j in (3, 5):
-                    finish(waiting[:2])
-                    waiting = waiting[2:]
+                if waiting and not last and j == TURN_AFTER:
+                    finish(waiting)
             if last:
-                finish(waiting[:2])
-                finish(waiting[2:])
+                finish(waiting)
                 tail = [tuple(units[0:2]), tuple(units[2:4]), (units[4],), (units[5],)]
                 for unit in units:
                     take_exp(unit)
+                    if unit < units[-1]:
+                        store_y(unit)
                     round_y(unit)
-                    for b, batch in enumerate(tail):
+                    for batch in tail:
                         if batch[-1] == unit:
-                            turn(batch, b)
-                    store_y(unit)
+                            turn(batch)
+                store_y(units[-1])
                 for batch in tail:
                     gather(batch, True)
                     quantise_y(batch)

@@ -29,7 +29,6 @@ ROWS = 4
 FIRST = 6
 GROUP = 6
 BANKS = 8
-TURN_AFTER = 4
 WARM = 7
 VECTOR_COLS = 336
 
@@ -93,10 +92,10 @@ def tile_endogenous_gridpoint_euler_step_k3_kernel(
             src = slump[P * PACK * g : P * PACK * (g + 1), WIDE * h : WIDE * (h + 1)]
             nc.sync.dma_start(out=slump_raw[h, g][:], in_=src.rearrange("(p j) n -> p j n", j=PACK))
 
-        def load_scales(queue, plane, scales):
+        def load_scales(plane, scales, which):
             rows = scales.rearrange("g (q r) n -> r q g n", r=ROWS)
-            for r in range(ROWS):
-                queue.dma_start(out=words(plane[r:P:32, :, :]), in_=words(rows[r]))
+            for r in which:
+                nc.sync.dma_start(out=words(plane[r:P:32, :, :]), in_=words(rows[r]))
 
         def interleave_slump(h, g, shared):
             grouped = flow.tile([P, WIDE, PACK], BF16, name="slump_grouped", align_bytes=64)
@@ -174,7 +173,7 @@ def tile_endogenous_gridpoint_euler_step_k3_kernel(
 
         def store_y(unit):
             h, i = divmod(unit, M_TILES)
-            y = flow.tile([P, WIDE], F32, name="y", bufs=6)
+            y = flow.tile([P, WIDE], F32, name="y", bufs=12)
             nc.vector.tensor_scalar(out=y[:], in0=cons[unit][:], scalar1=sav_col[:, i : i + 1], scalar2=None, op0=ADD)
             nc.sync.dma_start(out=out_0[P * i : P * (i + 1), WIDE * h : WIDE * (h + 1)], in_=y[:])
 
@@ -185,6 +184,31 @@ def tile_endogenous_gridpoint_euler_step_k3_kernel(
                 for u in range(2):
                     s = 2 * a + u
                     nc.tensor.transpose(turned[batch][:, P * s : P * (s + 1)], src[:, P * u : P * (u + 1)], ident[:])
+
+        def turn_blocks(batch):
+            turned[batch] = flow.tile([P, WIDE], F32, name="y_blocks", bufs=3, align_bytes=64)
+            src = halfs[batch[0] // 2][:].rearrange("m a u p e -> m (a u p e)").bitcast(F32)
+            nc.vector.transpose(out=turned[batch][:], in_=src)
+
+        def store_blocks():
+            codes = words(y_code[:, 0, :]).rearrange("p (t b j) -> p t b j", b=QUADS, j=32)
+            code_dst = words(out_1[0].rearrange("p m t -> p (m t)")).rearrange("(b i) (t q j) -> q i t b j", b=QUADS, q=QUADS, j=32)
+            scales = words(y_scale[:, 0, :]).rearrange("p (t b j) -> p t b j", b=QUADS, j=8)
+            scale_dst = words(out_2[0]).rearrange("(b r) (t q j) -> q r t b j", r=ROWS, q=QUADS, j=8)
+            for q in range(QUADS):
+                nc.sync.dma_start(out=code_dst[q], in_=codes[32 * q : 32 * (q + 1)])
+            for q in range(QUADS):
+                nc.sync.dma_start(out=scale_dst[q], in_=scales[32 * q : 32 * q + ROWS])
+
+        def finish_blocks(batches):
+            turn_blocks(batches[0])
+            for b, batch in enumerate(batches):
+                if b + 1 < len(batches):
+                    turn_blocks(batches[b + 1])
+                gather(batch, False)
+                if b > 0:
+                    quantise_y(batches[b - 1])
+            quantise_y(batches[-1])
 
         def gather(batch, on_scalar):
             count = len(batch)
@@ -200,6 +224,8 @@ def tile_endogenous_gridpoint_euler_step_k3_kernel(
             h, i = divmod(batch[0], M_TILES)
             cols = slice(P * i, P * (i + len(batch)))
             nc.vector.quantize_mx(out=y_code[:, h, cols].bitcast(FP8X4), scales=y_scale[:, h, cols], in_=packed[batch][:])
+            if h == 0:
+                return
             if batch[-1] % 2 == 1:
                 lo = cols.stop - 2 * P
                 dst = out_1[h].rearrange("p m t -> p (m t)")[:, PACK * lo : PACK * cols.stop]
@@ -207,8 +233,7 @@ def tile_endogenous_gridpoint_euler_step_k3_kernel(
             if cols.stop == M:
                 rows = out_2[h].rearrange("(q r) m -> r q m", r=ROWS)
                 for r in range(ROWS):
-                    queue = nc.scalar if h == HALVES - 1 and r % 2 == 0 else nc.sync
-                    queue.dma_start(out=words(rows[r]), in_=words(y_scale[r:P:32, h, :]))
+                    nc.sync.dma_start(out=words(rows[r]), in_=words(y_scale[r:P:32, h, :]))
 
         def finish(batches):
             for batch in batches:
@@ -228,20 +253,21 @@ def tile_endogenous_gridpoint_euler_step_k3_kernel(
         nc.vector.memset(words(u_scale[1][:]), 0)
         nc.vector.memset(words(calm_scale[1][:]), 0)
 
-        load_scales(nc.scalar, u_scale[0], u_scales[:, :, :split])
         nc.scalar.activation(out=spare[:], in_=one[:], func=ACT.Ln)
+        load_scales(u_scale[0], u_scales[:, :, :split], range(ROWS))
+        load_scales(calm_scale[0], calm_scales[:, :, :WIDE], range(2))
         load_u_codes(0, slice(0, 1))
         load_calm_codes(0)
-        load_scales(nc.sync, calm_scale[0], calm_scales[:, :, :WIDE])
+        load_scales(calm_scale[0], calm_scales[:, :, :WIDE], range(2, ROWS))
         load_u_codes(0, slice(1, 2))
         load_boom_codes(0)
         load_slump(0, 0)
-        load_scales(nc.sync, boom_scale, boom_scales)
+        load_scales(boom_scale, boom_scales, range(ROWS))
         load_slump(0, 1)
         nc.gpsimd.dma_start(out=sav_rows[:M_TILES, :], in_=sav.rearrange("(i p) -> i p", p=P))
         load_u_codes(1, slice(0, PASSES))
-        load_scales(nc.sync, u_scale[1], u_scales[:, :, split:])
-        load_scales(nc.sync, calm_scale[1], calm_scales[:, :, WIDE:])
+        load_scales(u_scale[1], u_scales[:, :, split:], range(ROWS))
+        load_scales(calm_scale[1], calm_scales[:, :, WIDE:], range(ROWS))
         load_calm_codes(1)
         load_boom_codes(1)
         load_slump(1, 0)
@@ -274,12 +300,10 @@ def tile_endogenous_gridpoint_euler_step_k3_kernel(
         for k in range(groups):
             units = range(k * GROUP, (k + 1) * GROUP)
             last = k == groups - 1
-            for j, unit in enumerate(units):
+            for unit in units:
                 if unit >= FIRST:
                     multiply(unit)
                     take_log(unit)
-                if waiting and not last and j == TURN_AFTER:
-                    finish(waiting)
             if last:
                 finish(waiting)
                 tail = [tuple(units[0:2]), tuple(units[2:4]), (units[4],), (units[5],)]
@@ -303,3 +327,7 @@ def tile_endogenous_gridpoint_euler_step_k3_kernel(
                 waiting = [(unit - 1, unit) for unit in units[1::2]]
                 if k == 0:
                     quantise_slump(1, 1, interleave_slump(1, 1, False))
+                if units[-1] < M_TILES:
+                    finish_blocks(waiting)
+                if units[-1] == M_TILES - 1:
+                    store_blocks()

@@ -19,18 +19,24 @@ ADD = mybir.AluOpType.add
 
 P = 128
 PACK = 4
-PASSES = K // (P * PACK)
+QUADRANT = 32
+SCALE_ROWS = 4
+BANKS = 8
 WIDE = 512
+PASSES = K // (P * PACK)
 HALVES = N // WIDE
 M_TILES = M // P
 UNITS = HALVES * M_TILES
-QUADS = 4
-ROWS = 4
+GROUPS = (9, 9, 6)
+PAIRS_HELD = max(GROUPS) // 2 + 2
+LATE_BATCHES = 3
+LATE_UNITS = 2
+CODE_RUN = 512
 FIRST = 6
-GROUP = 6
-BANKS = 8
-WARM = 7
+EARLY_ROWS = 2
+WARM_UPS = 7
 VECTOR_COLS = 336
+SAV_COLS = 16
 
 
 def tile_endogenous_gridpoint_euler_step_k3_kernel(
@@ -43,90 +49,84 @@ def tile_endogenous_gridpoint_euler_step_k3_kernel(
         psum = ctx.enter_context(tc.psum_pool(name="psum", bufs=BANKS))
         ctx.enter_context(tc.manual_schedule())
 
-        split = FIRST * P
-        u_spans = [(0, split), (split, M)]
-        u_code = [keep.tile([P, PASSES, b - a], U32, name="u_code%d" % i, align_bytes=64) for i, (a, b) in enumerate(u_spans)]
-        u_scale = [keep.tile([P, PASSES, b - a], U8, name="u_scale%d" % i, align_bytes=64) for i, (a, b) in enumerate(u_spans)]
-        calm_code = [keep.tile([P, PASSES, 2 * WIDE], U8, name="calm_code%d" % h, align_bytes=64) for h in range(HALVES)]
-        boom_code = [keep.tile([P, PASSES, WIDE], U32, name="boom_code%d" % h, align_bytes=64) for h in range(HALVES)]
-        calm_scale = [keep.tile([P, PASSES, WIDE], U8, name="calm_scale%d" % h, align_bytes=64) for h in range(HALVES)]
-        boom_scale = keep.tile([P, PASSES, N], U8, align_bytes=64)
-        slump_raw = {}
-        slump_code = {}
-        slump_scale = {}
-        for h in range(HALVES):
-            for g in range(PASSES):
-                slump_raw[h, g] = keep.tile([P, PACK, WIDE], BF16, name="slump_raw%d%d" % (h, g), align_bytes=64)
-                slump_code[h, g] = keep.tile([P, WIDE], U32, name="slump_code%d%d" % (h, g), align_bytes=64)
-                slump_scale[h, g] = keep.tile([P, WIDE], U8, name="slump_scale%d%d" % (h, g), align_bytes=64)
-        y_code = keep.tile([P, HALVES, M], U32, align_bytes=64)
-        y_scale = keep.tile([P, HALVES, M], U8, align_bytes=64)
-        ident = keep.tile([P, P], F32, align_bytes=64)
-        picker = keep.tile([P, 16], BF16, align_bytes=64)
-        sav_rows = keep.tile([P, P], BF16, align_bytes=64)
-        sav_col = keep.tile([P, 16], F32, align_bytes=64)
-        zeros = keep.tile([P, WIDE], BF16, align_bytes=64)
-        one = keep.tile([P, 1], F32, align_bytes=64)
-        spare = keep.tile([P, 1], F32, align_bytes=64)
+        def kept(name, shape, dtype):
+            return keep.tile(shape, dtype, name=name, align_bytes=64)
 
         def bank():
             return psum.tile([P, WIDE], F32, name="bank")
 
-        def words(ap):
+        def raw(ap):
             return ap.bitcast(I32)
 
-        def load_u_codes(i, passes):
-            a, b = u_spans[i]
+        split = FIRST * P
+        u_spans = [(0, split), (split, M)]
+        u_code = [kept("u_code%d" % i, [P, PASSES, b - a], U32) for i, (a, b) in enumerate(u_spans)]
+        u_scale = [kept("u_scale%d" % i, [P, PASSES, b - a], U8) for i, (a, b) in enumerate(u_spans)]
+        calm_code = [kept("calm_code%d" % h, [P, PASSES, 2 * WIDE], U8) for h in range(HALVES)]
+        calm_scale = [kept("calm_scale%d" % h, [P, PASSES, WIDE], U8) for h in range(HALVES)]
+        boom_code = [kept("boom_code%d" % h, [P, PASSES, WIDE], U32) for h in range(HALVES)]
+        boom_scale = kept("boom_scale", [P, PASSES, N], U8)
+        slabs = [(h, g) for h in range(HALVES) for g in range(PASSES)]
+        slump_rows = {s: kept("slump_rows%d%d" % s, [P, PACK, WIDE], BF16) for s in slabs}
+        slump_code = {s: kept("slump_code%d%d" % s, [P, WIDE], U32) for s in slabs}
+        slump_scale = {s: kept("slump_scale%d%d" % s, [P, WIDE], U8) for s in slabs}
+        y_code = kept("y_code", [P, HALVES, M], U32)
+        y_scale = kept("y_scale", [P, HALVES, M], U8)
+        ident = kept("ident", [P, P], F32)
+        picker = kept("picker", [P, SAV_COLS], BF16)
+        sav_rows = kept("sav_rows", [P, P], BF16)
+        sav_col = kept("sav_col", [P, SAV_COLS], F32)
+        zeros = kept("zeros", [P, WIDE], BF16)
+
+        def load_u_codes(part, passes):
+            a, b = u_spans[part]
             src = u_words.rearrange("g p m t -> p g (m t)")[:, passes, PACK * a : PACK * b]
-            nc.sync.dma_start(out=words(u_code[i][:, passes, :]), in_=words(src))
+            nc.sync.dma_start(out=raw(u_code[part][:, passes, :]), in_=raw(src))
 
         def load_calm_codes(h):
             src = calm_words.rearrange("g p b -> p g b")[:, :, 2 * WIDE * h : 2 * WIDE * (h + 1)]
-            nc.sync.dma_start(out=words(calm_code[h][:]), in_=words(src))
+            nc.sync.dma_start(out=raw(calm_code[h][:]), in_=raw(src))
 
         def load_boom_codes(h):
             src = boom_words.rearrange("g p n t -> p g (n t)")[:, :, PACK * WIDE * h : PACK * WIDE * (h + 1)]
-            nc.sync.dma_start(out=words(boom_code[h][:]), in_=words(src))
+            nc.sync.dma_start(out=raw(boom_code[h][:]), in_=raw(src))
 
         def load_slump(h, g):
             src = slump[P * PACK * g : P * PACK * (g + 1), WIDE * h : WIDE * (h + 1)]
-            nc.sync.dma_start(out=slump_raw[h, g][:], in_=src.rearrange("(p j) n -> p j n", j=PACK))
+            nc.sync.dma_start(out=slump_rows[h, g][:], in_=src.rearrange("(p t) n -> p t n", t=PACK))
 
-        def load_scales(plane, scales, which):
-            rows = scales.rearrange("g (q r) n -> r q g n", r=ROWS)
+        def load_scales(tile, scales, which):
+            rows = scales.rearrange("g (quad r) n -> r quad g n", r=SCALE_ROWS)
             for r in which:
-                nc.sync.dma_start(out=words(plane[r:P:32, :, :]), in_=words(rows[r]))
+                nc.sync.dma_start(out=raw(tile[r:P:QUADRANT, :, :]), in_=raw(rows[r]))
 
-        def interleave_slump(h, g, shared):
+        def quantise_slump(h, g, vector_cols):
             grouped = flow.tile([P, WIDE, PACK], BF16, name="slump_grouped", align_bytes=64)
-            src = slump_raw[h, g][:].rearrange("p j n -> p n j")
-            cut = VECTOR_COLS if shared else WIDE
-            nc.vector.tensor_copy(out=grouped[:, :cut, :], in_=src[:, :cut, :])
-            if shared:
-                nc.scalar.copy(out=grouped[:, cut:, :], in_=src[:, cut:, :])
-            return grouped
-
-        def quantise_slump(h, g, grouped):
+            src = slump_rows[h, g][:].rearrange("p t n -> p n t")
+            nc.vector.tensor_copy(out=grouped[:, :vector_cols, :], in_=src[:, :vector_cols, :])
+            if vector_cols < WIDE:
+                nc.scalar.copy(out=grouped[:, vector_cols:, :], in_=src[:, vector_cols:, :])
             nc.vector.quantize_mx(
                 out=slump_code[h, g][:].bitcast(FP8X4),
                 scales=slump_scale[h, g][:],
-                in_=grouped[:].rearrange("p n j -> p (n j)"),
+                in_=grouped[:].rearrange("p n t -> p (n t)"),
             )
 
-        sums = {}
+        steps = [(regime, g) for regime in ("calm", "boom", "slump") for g in range(PASSES)]
+        sums, logs, cons, rounded, turned, packed = {}, {}, {}, {}, {}, {}
 
-        def one_pass(unit, regime, g, start, stop):
+        def one_pass(unit, step):
+            regime, g = steps[step]
             h, i = divmod(unit, M_TILES)
             part = 0 if i < FIRST else 1
             lo = i * P - u_spans[part][0]
-            cols = slice(WIDE * h, WIDE * (h + 1))
             if regime == "calm":
                 rhs, rhs_scale = calm_code[h][:, g, :].bitcast(FP4X4), calm_scale[h][:, g, :]
             elif regime == "boom":
-                rhs, rhs_scale = boom_code[h][:, g, :].bitcast(FP8X4), boom_scale[:, g, cols]
+                rhs, rhs_scale = boom_code[h][:, g, :].bitcast(FP8X4), boom_scale[:, g, WIDE * h : WIDE * (h + 1)]
             else:
                 rhs, rhs_scale = slump_code[h, g][:].bitcast(FP8X4), slump_scale[h, g][:]
-            if start:
+            if step == 0:
                 sums[unit] = bank()
             nc.tensor.matmul_mx(
                 out=sums[unit][:],
@@ -134,140 +134,98 @@ def tile_endogenous_gridpoint_euler_step_k3_kernel(
                 lhsT_scale=u_scale[part][:, g, lo : lo + P],
                 rhs=rhs,
                 rhs_scale=rhs_scale,
-                start=start,
-                stop=stop,
+                start=step == 0,
+                stop=step == len(steps) - 1,
             )
-
-        steps = [(regime, g) for regime in ("calm", "boom", "slump") for g in range(PASSES)]
-
-        def multiply(unit):
-            for s, (regime, g) in enumerate(steps):
-                one_pass(unit, regime, g, s == 0, s == len(steps) - 1)
-
-        logs = {}
-        cons = {}
-        halfs = {}
-        turned = {}
-        packed = {}
 
         def take_log(unit):
-            logs[unit] = flow.tile([P, WIDE], F32, name="log_e", bufs=GROUP + 1)
-            nc.scalar.activation(out=logs[unit][:], in_=sums[unit][:], func=ACT.Ln)
-
-        def take_exp(unit):
-            cons[unit] = flow.tile([P, WIDE], F32, name="cons", bufs=GROUP)
-            nc.scalar.activation(out=cons[unit][:], in_=logs[unit][:], func=ACT.Exp, scale=-1.0 / GAMMA)
-
-        def round_y(unit):
             pair, a = divmod(unit, 2)
-            i = unit % M_TILES
             if a == 0:
-                halfs[pair] = flow.tile([P, 2, 2, P, 2], BF16, name="y_bf16", bufs=6, align_bytes=64)
-            nc.vector.tensor_scalar(
-                out=halfs[pair][:, a],
-                in0=cons[unit][:].rearrange("m (p u e) -> m u p e", u=2, e=2),
-                scalar1=sav_col[:, i : i + 1],
-                scalar2=None,
-                op0=ADD,
-            )
+                logs[pair] = flow.tile([P, 2, WIDE], F32, name="log_e", bufs=PAIRS_HELD)
+            nc.scalar.activation(out=logs[pair][:, a, :], in_=sums[unit][:], func=ACT.Ln)
+
+        def take_exp(batch):
+            pair, a = divmod(batch[0], 2)
+            if a == 0:
+                cons[pair] = flow.tile([P, 2, WIDE], F32, name="consumption", bufs=PAIRS_HELD)
+            span = slice(a, a + len(batch))
+            nc.scalar.activation(out=cons[pair][:, span, :], in_=logs[pair][:, span, :], func=ACT.Exp, scale=-1.0 / GAMMA)
+
+        def add_sav(unit, out, in0):
+            i = unit % M_TILES
+            nc.vector.tensor_scalar(out=out, in0=in0, scalar1=sav_col[:, i : i + 1], scalar2=None, op0=ADD)
 
         def store_y(unit):
             h, i = divmod(unit, M_TILES)
-            y = flow.tile([P, WIDE], F32, name="y", bufs=12)
-            nc.vector.tensor_scalar(out=y[:], in0=cons[unit][:], scalar1=sav_col[:, i : i + 1], scalar2=None, op0=ADD)
+            y = flow.tile([P, WIDE], F32, name="y", bufs=max(GROUPS))
+            add_sav(unit, y[:], cons[unit // 2][:, unit % 2, :])
             nc.sync.dma_start(out=out_0[P * i : P * (i + 1), WIDE * h : WIDE * (h + 1)], in_=y[:])
+
+        def round_y(unit):
+            pair, a = divmod(unit, 2)
+            if a == 0:
+                rounded[pair] = flow.tile([P, 2, 2, P, 2], BF16, name="y_bf16", bufs=2 * PAIRS_HELD, align_bytes=64)
+            src = cons[pair][:, a, :].rearrange("m (p u e) -> m u p e", u=2, e=2)
+            add_sav(unit, rounded[pair][:, a], src)
 
         def turn(batch):
             turned[batch] = bank()
             for a, unit in enumerate(batch):
-                src = halfs[unit // 2][:, unit % 2].rearrange("m u p e -> m (u p e)").bitcast(F32)
+                src = rounded[unit // 2][:, unit % 2].rearrange("m u p e -> m (u p e)").bitcast(F32)
                 for u in range(2):
-                    s = 2 * a + u
-                    nc.tensor.transpose(turned[batch][:, P * s : P * (s + 1)], src[:, P * u : P * (u + 1)], ident[:])
+                    slot = 2 * a + u
+                    nc.tensor.transpose(turned[batch][:, P * slot : P * (slot + 1)], src[:, P * u : P * (u + 1)], ident[:])
 
-        def turn_blocks(batch):
-            turned[batch] = flow.tile([P, WIDE], F32, name="y_blocks", bufs=3, align_bytes=64)
-            src = halfs[batch[0] // 2][:].rearrange("m a u p e -> m (a u p e)").bitcast(F32)
-            nc.vector.transpose(out=turned[batch][:], in_=src)
-
-        def store_blocks():
-            codes = words(y_code[:, 0, :]).rearrange("p (t b j) -> p t b j", b=QUADS, j=32)
-            code_dst = words(out_1[0].rearrange("p m t -> p (m t)")).rearrange("(b i) (t q j) -> q i t b j", b=QUADS, q=QUADS, j=32)
-            scales = words(y_scale[:, 0, :]).rearrange("p (t b j) -> p t b j", b=QUADS, j=8)
-            scale_dst = words(out_2[0]).rearrange("(b r) (t q j) -> q r t b j", r=ROWS, q=QUADS, j=8)
-            for q in range(QUADS):
-                nc.sync.dma_start(out=code_dst[q], in_=codes[32 * q : 32 * (q + 1)])
-            for q in range(QUADS):
-                nc.sync.dma_start(out=scale_dst[q], in_=scales[32 * q : 32 * q + ROWS])
-
-        def finish_blocks(batches):
-            turn_blocks(batches[0])
-            for b, batch in enumerate(batches):
-                if b + 1 < len(batches):
-                    turn_blocks(batches[b + 1])
-                gather(batch, False)
-                if b > 0:
-                    quantise_y(batches[b - 1])
-            quantise_y(batches[-1])
-
-        def gather(batch, on_scalar):
+        def gather(batch, copy):
             count = len(batch)
-            packed[batch] = flow.tile([P, count * P * PACK], BF16, name="y_packed", bufs=4, align_bytes=64)
+            packed[batch] = flow.tile([P, count * P * PACK], BF16, name="y_packed", bufs=PAIRS_HELD, align_bytes=64)
             dst = packed[batch][:].bitcast(F32).rearrange("p (a m u) -> p a m u", a=count, u=2)
-            src = turned[batch][:, : count * 2 * P].rearrange("p (a u m) -> p a m u", a=count, u=2)
-            if on_scalar:
-                nc.scalar.copy(out=dst, in_=src)
-            else:
-                nc.vector.tensor_copy(out=dst, in_=src)
+            copy(out=dst, in_=turned[batch][:, : count * 2 * P].rearrange("p (a u m) -> p a m u", a=count, u=2))
 
         def quantise_y(batch):
             h, i = divmod(batch[0], M_TILES)
-            cols = slice(P * i, P * (i + len(batch)))
-            nc.vector.quantize_mx(out=y_code[:, h, cols].bitcast(FP8X4), scales=y_scale[:, h, cols], in_=packed[batch][:])
-            if h == 0:
-                return
-            if batch[-1] % 2 == 1:
-                lo = cols.stop - 2 * P
-                dst = out_1[h].rearrange("p m t -> p (m t)")[:, PACK * lo : PACK * cols.stop]
-                nc.sync.dma_start(out=words(dst), in_=words(y_code[:, h, lo : cols.stop]))
-            if cols.stop == M:
-                rows = out_2[h].rearrange("(q r) m -> r q m", r=ROWS)
-                for r in range(ROWS):
-                    nc.sync.dma_start(out=words(rows[r]), in_=words(y_scale[r:P:32, h, :]))
+            lo, hi = P * i, P * (i + len(batch))
+            nc.vector.quantize_mx(out=y_code[:, h, lo:hi].bitcast(FP8X4), scales=y_scale[:, h, lo:hi], in_=packed[batch][:])
+            if hi % CODE_RUN == 0:
+                dst = out_1[h].rearrange("p m t -> p (m t)")[:, PACK * (hi - CODE_RUN) : PACK * hi]
+                nc.sync.dma_start(out=raw(dst), in_=raw(y_code[:, h, hi - CODE_RUN : hi]))
+            if hi == M:
+                rows = out_2[h].rearrange("(quad r) m -> r quad m", r=SCALE_ROWS)
+                for r in range(SCALE_ROWS):
+                    nc.sync.dma_start(out=raw(rows[r]), in_=raw(y_scale[r:P:QUADRANT, h, :]))
 
-        def finish(batches):
+        def make_planes(batches):
             for batch in batches:
                 turn(batch)
             for b, batch in enumerate(batches):
-                gather(batch, False)
+                gather(batch, nc.vector.tensor_copy)
                 if b > 0:
                     quantise_y(batches[b - 1])
             quantise_y(batches[-1])
 
-        nc.gpsimd.memset(words(u_scale[0][:]), 0)
-        nc.vector.memset(words(calm_scale[0][:]), 0)
+        nc.gpsimd.memset(raw(u_scale[0][:]), 0)
+        nc.vector.memset(raw(calm_scale[0][:]), 0)
         nc.vector.memset(zeros[:], 0.0)
-        nc.vector.memset(one[:], 1.0)
-        nc.vector.memset(words(boom_scale[:]), 0)
+        nc.vector.memset(raw(boom_scale[:]), 0)
         nc.vector.memset(sav_rows[:], 0.0)
-        nc.vector.memset(words(u_scale[1][:]), 0)
-        nc.vector.memset(words(calm_scale[1][:]), 0)
+        nc.vector.memset(raw(u_scale[1][:]), 0)
+        nc.vector.memset(raw(calm_scale[1][:]), 0)
 
-        nc.scalar.activation(out=spare[:], in_=one[:], func=ACT.Ln)
-        load_scales(u_scale[0], u_scales[:, :, :split], range(ROWS))
-        load_scales(calm_scale[0], calm_scales[:, :, :WIDE], range(2))
+        all_rows = range(SCALE_ROWS)
+        load_scales(u_scale[0], u_scales[:, :, :split], all_rows)
+        load_scales(calm_scale[0], calm_scales[:, :, :WIDE], all_rows[:EARLY_ROWS])
         load_u_codes(0, slice(0, 1))
         load_calm_codes(0)
-        load_scales(calm_scale[0], calm_scales[:, :, :WIDE], range(2, ROWS))
-        load_u_codes(0, slice(1, 2))
+        load_scales(calm_scale[0], calm_scales[:, :, :WIDE], all_rows[EARLY_ROWS:])
+        load_u_codes(0, slice(1, PASSES))
         load_boom_codes(0)
         load_slump(0, 0)
-        load_scales(boom_scale, boom_scales, range(ROWS))
+        load_scales(boom_scale, boom_scales, all_rows)
         load_slump(0, 1)
         nc.gpsimd.dma_start(out=sav_rows[:M_TILES, :], in_=sav.rearrange("(i p) -> i p", p=P))
         load_u_codes(1, slice(0, PASSES))
-        load_scales(u_scale[1], u_scales[:, :, split:], range(ROWS))
-        load_scales(calm_scale[1], calm_scales[:, :, WIDE:], range(ROWS))
+        load_scales(u_scale[1], u_scales[:, :, split:], all_rows)
+        load_scales(calm_scale[1], calm_scales[:, :, WIDE:], all_rows)
         load_calm_codes(1)
         load_boom_codes(1)
         load_slump(1, 0)
@@ -275,59 +233,63 @@ def tile_endogenous_gridpoint_euler_step_k3_kernel(
         make_identity(nc, ident[:])
 
         warm = bank()
-        for w in range(WARM):
+        for step in range(WARM_UPS):
             nc.tensor.matmul(warm[:], lhsT=zeros[:, :P], rhs=zeros[:], start=True, stop=True)
 
         for g in range(PASSES):
-            quantise_slump(0, g, interleave_slump(0, g, True))
-        nc.vector.tensor_copy(out=picker[:], in_=ident[:, :16])
+            quantise_slump(0, g, VECTOR_COLS)
+        nc.vector.tensor_copy(out=picker[:], in_=ident[:, :SAV_COLS])
 
-        for s, (regime, g) in enumerate(steps[:-PASSES]):
+        given = len(steps) - PASSES
+        for step in range(given):
             for unit in range(FIRST):
-                one_pass(unit, regime, g, s == 0, False)
+                one_pass(unit, step)
         for unit in range(FIRST):
-            for g in range(PASSES):
-                one_pass(unit, "slump", g, False, g == PASSES - 1)
+            for step in range(given, len(steps)):
+                one_pass(unit, step)
             take_log(unit)
+
         spread = bank()
-        nc.tensor.matmul(spread[:, :16], lhsT=sav_rows[:], rhs=picker[:], start=True, stop=True)
-        nc.vector.tensor_copy(out=sav_col[:], in_=spread[:, :16])
+        nc.tensor.matmul(spread[:, :SAV_COLS], lhsT=sav_rows[:], rhs=picker[:], start=True, stop=True)
+        nc.vector.tensor_copy(out=sav_col[:], in_=spread[:, :SAV_COLS])
 
-        quantise_slump(1, 0, interleave_slump(1, 0, False))
+        for g in range(PASSES):
+            quantise_slump(1, g, WIDE)
 
-        groups = UNITS // GROUP
         waiting = []
-        for k in range(groups):
-            units = range(k * GROUP, (k + 1) * GROUP)
-            last = k == groups - 1
+        begin = 0
+        for size in GROUPS:
+            units = range(begin, begin + size)
+            begin += size
+            batches = [tuple(unit for unit in units if unit // 2 == pair) for pair in range(units[0] // 2, units[-1] // 2 + 1)]
             for unit in units:
                 if unit >= FIRST:
-                    multiply(unit)
+                    for step in range(len(steps)):
+                        one_pass(unit, step)
                     take_log(unit)
-            if last:
-                finish(waiting)
-                tail = [tuple(units[0:2]), tuple(units[2:4]), (units[4],), (units[5],)]
-                for unit in units:
-                    take_exp(unit)
-                    if unit < units[-1]:
+                if unit == UNITS - 1 - LATE_UNITS:
+                    make_planes(waiting[:-LATE_BATCHES])
+                    waiting = waiting[-LATE_BATCHES:]
+            if waiting:
+                make_planes(waiting)
+            if begin < UNITS:
+                for batch in batches:
+                    take_exp(batch)
+                    for unit in batch:
+                        round_y(unit)
                         store_y(unit)
-                    round_y(unit)
-                    for batch in tail:
-                        if batch[-1] == unit:
-                            turn(batch)
-                store_y(units[-1])
-                for batch in tail:
-                    gather(batch, True)
-                    quantise_y(batch)
-            else:
-                for unit in units:
-                    take_exp(unit)
-                    round_y(unit)
-                    store_y(unit)
-                waiting = [(unit - 1, unit) for unit in units[1::2]]
-                if k == 0:
-                    quantise_slump(1, 1, interleave_slump(1, 1, False))
-                if units[-1] < M_TILES:
-                    finish_blocks(waiting)
-                if units[-1] == M_TILES - 1:
-                    store_blocks()
+                waiting = batches
+
+        batches = batches[:-1] + [(unit,) for unit in batches[-1]]
+        for unit in units:
+            take_exp((unit,))
+            if unit < units[-1]:
+                store_y(unit)
+            round_y(unit)
+            for batch in batches:
+                if batch[-1] == unit:
+                    turn(batch)
+        store_y(units[-1])
+        for batch in batches:
+            gather(batch, nc.scalar.copy)
+            quantise_y(batch)

from contextlib import ExitStack

import concourse.mybir as mybir
from concourse.masks import make_identity

M, K, N = 1536, 1024, 1024
GAMMA = 1.5
FLOPS = 3 * 2 * M * K * N

F32 = mybir.dt.float32
BF16 = mybir.dt.bfloat16
I32 = mybir.dt.int32
U32 = mybir.dt.uint32
U8 = mybir.dt.uint8
FP8X4 = mybir.dt.float8_e4m3fn_x4
FP4X4 = mybir.dt.float4_e2m1fn_x4
ACT = mybir.ActivationFunctionType
ADD = mybir.AluOpType.add

P = 128
PACK = 4
QUADRANT = 32
SCALE_ROWS = 4
BANKS = 8
WIDE = 512
PASSES = K // (P * PACK)
HALVES = N // WIDE
M_TILES = M // P
UNITS = HALVES * M_TILES
GROUPS = (9, 9, 6)
PAIRS_HELD = max(GROUPS) // 2 + 2
LATE_BATCHES = 3
LATE_UNITS = 2
CODE_RUN = 512
FIRST = 6
EARLY_ROWS = 2
WARM_UPS = 7
VECTOR_COLS = 336
SAV_COLS = 16


def tile_endogenous_gridpoint_euler_step_k3_kernel(
    tc, u_words, u_scales, calm_words, calm_scales, boom_words, boom_scales, slump, sav, out_0, out_1, out_2
):
    nc = tc.nc
    with ExitStack() as ctx:
        keep = ctx.enter_context(tc.tile_pool(name="keep", bufs=1))
        flow = ctx.enter_context(tc.tile_pool(name="flow", bufs=2))
        psum = ctx.enter_context(tc.psum_pool(name="psum", bufs=BANKS))
        ctx.enter_context(tc.manual_schedule())

        def kept(name, shape, dtype):
            return keep.tile(shape, dtype, name=name, align_bytes=64)

        def bank():
            return psum.tile([P, WIDE], F32, name="bank")

        def raw(ap):
            return ap.bitcast(I32)

        split = FIRST * P
        u_spans = [(0, split), (split, M)]
        u_code = [kept("u_code%d" % i, [P, PASSES, b - a], U32) for i, (a, b) in enumerate(u_spans)]
        u_scale = [kept("u_scale%d" % i, [P, PASSES, b - a], U8) for i, (a, b) in enumerate(u_spans)]
        calm_code = [kept("calm_code%d" % h, [P, PASSES, 2 * WIDE], U8) for h in range(HALVES)]
        calm_scale = [kept("calm_scale%d" % h, [P, PASSES, WIDE], U8) for h in range(HALVES)]
        boom_code = [kept("boom_code%d" % h, [P, PASSES, WIDE], U32) for h in range(HALVES)]
        boom_scale = kept("boom_scale", [P, PASSES, N], U8)
        slabs = [(h, g) for h in range(HALVES) for g in range(PASSES)]
        slump_rows = {s: kept("slump_rows%d%d" % s, [P, PACK, WIDE], BF16) for s in slabs}
        slump_code = {s: kept("slump_code%d%d" % s, [P, WIDE], U32) for s in slabs}
        slump_scale = {s: kept("slump_scale%d%d" % s, [P, WIDE], U8) for s in slabs}
        y_code = kept("y_code", [P, HALVES, M], U32)
        y_scale = kept("y_scale", [P, HALVES, M], U8)
        ident = kept("ident", [P, P], F32)
        picker = kept("picker", [P, SAV_COLS], BF16)
        sav_rows = kept("sav_rows", [P, P], BF16)
        sav_col = kept("sav_col", [P, SAV_COLS], F32)
        zeros = kept("zeros", [P, WIDE], BF16)

        def load_u_codes(part, passes):
            a, b = u_spans[part]
            src = u_words.rearrange("g p m t -> p g (m t)")[:, passes, PACK * a : PACK * b]
            nc.sync.dma_start(out=raw(u_code[part][:, passes, :]), in_=raw(src))

        def load_calm_codes(h):
            src = calm_words.rearrange("g p b -> p g b")[:, :, 2 * WIDE * h : 2 * WIDE * (h + 1)]
            nc.sync.dma_start(out=raw(calm_code[h][:]), in_=raw(src))

        def load_boom_codes(h):
            src = boom_words.rearrange("g p n t -> p g (n t)")[:, :, PACK * WIDE * h : PACK * WIDE * (h + 1)]
            nc.sync.dma_start(out=raw(boom_code[h][:]), in_=raw(src))

        def load_slump(h, g):
            src = slump[P * PACK * g : P * PACK * (g + 1), WIDE * h : WIDE * (h + 1)]
            nc.sync.dma_start(out=slump_rows[h, g][:], in_=src.rearrange("(p t) n -> p t n", t=PACK))

        def load_scales(tile, scales, which):
            rows = scales.rearrange("g (quad r) n -> r quad g n", r=SCALE_ROWS)
            for r in which:
                nc.sync.dma_start(out=raw(tile[r:P:QUADRANT, :, :]), in_=raw(rows[r]))

        def quantise_slump(h, g, vector_cols):
            grouped = flow.tile([P, WIDE, PACK], BF16, name="slump_grouped", align_bytes=64)
            src = slump_rows[h, g][:].rearrange("p t n -> p n t")
            nc.vector.tensor_copy(out=grouped[:, :vector_cols, :], in_=src[:, :vector_cols, :])
            if vector_cols < WIDE:
                nc.scalar.copy(out=grouped[:, vector_cols:, :], in_=src[:, vector_cols:, :])
            nc.vector.quantize_mx(
                out=slump_code[h, g][:].bitcast(FP8X4),
                scales=slump_scale[h, g][:],
                in_=grouped[:].rearrange("p n t -> p (n t)"),
            )

        steps = [(regime, g) for regime in ("calm", "boom", "slump") for g in range(PASSES)]
        sums, logs, cons, rounded, turned, packed = {}, {}, {}, {}, {}, {}

        def one_pass(unit, step):
            regime, g = steps[step]
            h, i = divmod(unit, M_TILES)
            part = 0 if i < FIRST else 1
            lo = i * P - u_spans[part][0]
            if regime == "calm":
                rhs, rhs_scale = calm_code[h][:, g, :].bitcast(FP4X4), calm_scale[h][:, g, :]
            elif regime == "boom":
                rhs, rhs_scale = boom_code[h][:, g, :].bitcast(FP8X4), boom_scale[:, g, WIDE * h : WIDE * (h + 1)]
            else:
                rhs, rhs_scale = slump_code[h, g][:].bitcast(FP8X4), slump_scale[h, g][:]
            if step == 0:
                sums[unit] = bank()
            nc.tensor.matmul_mx(
                out=sums[unit][:],
                lhsT=u_code[part][:, g, lo : lo + P].bitcast(FP8X4),
                lhsT_scale=u_scale[part][:, g, lo : lo + P],
                rhs=rhs,
                rhs_scale=rhs_scale,
                start=step == 0,
                stop=step == len(steps) - 1,
            )

        def take_log(unit):
            pair, a = divmod(unit, 2)
            if a == 0:
                logs[pair] = flow.tile([P, 2, WIDE], F32, name="log_e", bufs=PAIRS_HELD)
            nc.scalar.activation(out=logs[pair][:, a, :], in_=sums[unit][:], func=ACT.Ln)

        def take_exp(batch):
            pair, a = divmod(batch[0], 2)
            if a == 0:
                cons[pair] = flow.tile([P, 2, WIDE], F32, name="consumption", bufs=PAIRS_HELD)
            span = slice(a, a + len(batch))
            nc.scalar.activation(out=cons[pair][:, span, :], in_=logs[pair][:, span, :], func=ACT.Exp, scale=-1.0 / GAMMA)

        def add_sav(unit, out, in0):
            i = unit % M_TILES
            nc.vector.tensor_scalar(out=out, in0=in0, scalar1=sav_col[:, i : i + 1], scalar2=None, op0=ADD)

        def store_y(unit):
            h, i = divmod(unit, M_TILES)
            y = flow.tile([P, WIDE], F32, name="y", bufs=max(GROUPS))
            add_sav(unit, y[:], cons[unit // 2][:, unit % 2, :])
            nc.sync.dma_start(out=out_0[P * i : P * (i + 1), WIDE * h : WIDE * (h + 1)], in_=y[:])

        def round_y(unit):
            pair, a = divmod(unit, 2)
            if a == 0:
                rounded[pair] = flow.tile([P, 2, 2, P, 2], BF16, name="y_bf16", bufs=2 * PAIRS_HELD, align_bytes=64)
            src = cons[pair][:, a, :].rearrange("m (p u e) -> m u p e", u=2, e=2)
            add_sav(unit, rounded[pair][:, a], src)

        def turn(batch):
            turned[batch] = bank()
            for a, unit in enumerate(batch):
                src = rounded[unit // 2][:, unit % 2].rearrange("m u p e -> m (u p e)").bitcast(F32)
                for u in range(2):
                    slot = 2 * a + u
                    nc.tensor.transpose(turned[batch][:, P * slot : P * (slot + 1)], src[:, P * u : P * (u + 1)], ident[:])

        def gather(batch, copy):
            count = len(batch)
            packed[batch] = flow.tile([P, count * P * PACK], BF16, name="y_packed", bufs=PAIRS_HELD, align_bytes=64)
            dst = packed[batch][:].bitcast(F32).rearrange("p (a m u) -> p a m u", a=count, u=2)
            copy(out=dst, in_=turned[batch][:, : count * 2 * P].rearrange("p (a u m) -> p a m u", a=count, u=2))

        def quantise_y(batch):
            h, i = divmod(batch[0], M_TILES)
            lo, hi = P * i, P * (i + len(batch))
            nc.vector.quantize_mx(out=y_code[:, h, lo:hi].bitcast(FP8X4), scales=y_scale[:, h, lo:hi], in_=packed[batch][:])
            if hi % CODE_RUN == 0:
                dst = out_1[h].rearrange("p m t -> p (m t)")[:, PACK * (hi - CODE_RUN) : PACK * hi]
                nc.sync.dma_start(out=raw(dst), in_=raw(y_code[:, h, hi - CODE_RUN : hi]))
            if hi == M:
                rows = out_2[h].rearrange("(quad r) m -> r quad m", r=SCALE_ROWS)
                for r in range(SCALE_ROWS):
                    nc.sync.dma_start(out=raw(rows[r]), in_=raw(y_scale[r:P:QUADRANT, h, :]))

        def make_planes(batches):
            for batch in batches:
                turn(batch)
            for b, batch in enumerate(batches):
                gather(batch, nc.vector.tensor_copy)
                if b > 0:
                    quantise_y(batches[b - 1])
            quantise_y(batches[-1])

        nc.gpsimd.memset(raw(u_scale[0][:]), 0)
        nc.vector.memset(raw(calm_scale[0][:]), 0)
        nc.vector.memset(zeros[:], 0.0)
        nc.vector.memset(raw(boom_scale[:]), 0)
        nc.vector.memset(sav_rows[:], 0.0)
        nc.vector.memset(raw(u_scale[1][:]), 0)
        nc.vector.memset(raw(calm_scale[1][:]), 0)

        all_rows = range(SCALE_ROWS)
        load_scales(u_scale[0], u_scales[:, :, :split], all_rows)
        load_scales(calm_scale[0], calm_scales[:, :, :WIDE], all_rows[:EARLY_ROWS])
        load_u_codes(0, slice(0, 1))
        load_calm_codes(0)
        load_scales(calm_scale[0], calm_scales[:, :, :WIDE], all_rows[EARLY_ROWS:])
        load_u_codes(0, slice(1, PASSES))
        load_boom_codes(0)
        load_slump(0, 0)
        load_scales(boom_scale, boom_scales, all_rows)
        load_slump(0, 1)
        nc.gpsimd.dma_start(out=sav_rows[:M_TILES, :], in_=sav.rearrange("(i p) -> i p", p=P))
        load_u_codes(1, slice(0, PASSES))
        load_scales(u_scale[1], u_scales[:, :, split:], all_rows)
        load_scales(calm_scale[1], calm_scales[:, :, WIDE:], all_rows)
        load_calm_codes(1)
        load_boom_codes(1)
        load_slump(1, 0)
        load_slump(1, 1)
        make_identity(nc, ident[:])

        warm = bank()
        for step in range(WARM_UPS):
            nc.tensor.matmul(warm[:], lhsT=zeros[:, :P], rhs=zeros[:], start=True, stop=True)

        for g in range(PASSES):
            quantise_slump(0, g, VECTOR_COLS)
        nc.vector.tensor_copy(out=picker[:], in_=ident[:, :SAV_COLS])

        given = len(steps) - PASSES
        for step in range(given):
            for unit in range(FIRST):
                one_pass(unit, step)
        for unit in range(FIRST):
            for step in range(given, len(steps)):
                one_pass(unit, step)
            take_log(unit)

        spread = bank()
        nc.tensor.matmul(spread[:, :SAV_COLS], lhsT=sav_rows[:], rhs=picker[:], start=True, stop=True)
        nc.vector.tensor_copy(out=sav_col[:], in_=spread[:, :SAV_COLS])

        for g in range(PASSES):
            quantise_slump(1, g, WIDE)

        waiting = []
        begin = 0
        for size in GROUPS:
            units = range(begin, begin + size)
            begin += size
            batches = [tuple(unit for unit in units if unit // 2 == pair) for pair in range(units[0] // 2, units[-1] // 2 + 1)]
            for unit in units:
                if unit >= FIRST:
                    for step in range(len(steps)):
                        one_pass(unit, step)
                    take_log(unit)
                if unit == UNITS - 1 - LATE_UNITS:
                    make_planes(waiting[:-LATE_BATCHES])
                    waiting = waiting[-LATE_BATCHES:]
            if waiting:
                make_planes(waiting)
            if begin < UNITS:
                for batch in batches:
                    take_exp(batch)
                    for unit in batch:
                        round_y(unit)
                        store_y(unit)
                waiting = batches

        batches = batches[:-1] + [(unit,) for unit in batches[-1]]
        for unit in units:
            take_exp((unit,))
            if unit < units[-1]:
                store_y(unit)
            round_y(unit)
            for batch in batches:
                if batch[-1] == unit:
                    turn(batch)
        store_y(units[-1])
        for batch in batches:
            gather(batch, nc.scalar.copy)
            quantise_y(batch)
